import numpy as np
import ml_dtypes


def mxq(x, axis, fmt="e4m3"):
    dtype, down = {"e4m3": (ml_dtypes.float8_e4m3fn, 7), "e5m2": (ml_dtypes.float8_e5m2, 14)}[fmt]
    v = np.moveaxis(np.asarray(x, np.float32).astype(ml_dtypes.bfloat16).astype(np.float64), axis, -1)
    blocks = v.reshape(v.shape[:-1] + (-1, 32))
    amax = np.abs(blocks).max(-1, keepdims=True)
    byte = np.maximum(np.where(amax > 0, np.frexp(amax)[1] - 1 + 127, 0) - down, 1)
    scale = np.exp2(byte - 127.0)
    codes = (blocks / scale).astype(np.float32).astype(dtype).astype(np.float64)
    return np.moveaxis((codes * scale).reshape(v.shape), -1, axis)


WIDE = False


def mx_kscale(k):
    if not WIDE:
        return np.ones(k)
    levels = np.array([10, -10, 5, -5, 0])
    if k % 512:
        return np.exp2(np.random.permutation(np.resize(levels, k // 32))).repeat(32)
    a = np.empty((k // 512, 16))
    for p in range(k // 512):
        a[p, :8] = np.random.permutation(np.resize(levels, 8))
        for g in range(8):
            far = levels[np.abs(levels - a[p, g]) >= 10]
            a[p, g + 8] = far[np.random.randint(len(far))]
    return np.exp2(a.ravel()).repeat(32)


def f64(x):
    return np.asarray(x).astype(np.float64)


def striped(idx):
    return np.tile(idx.reshape(-1, 16).T, (8, 1)).astype(np.uint16)


def unstriped(offs):
    return offs[:16].T.reshape(-1).astype(np.int64)


def striped8(idx):
    return np.concatenate([x.reshape(-1, 16).T for x in idx]).astype(np.uint16)


def runs(offs, k):
    lists = np.stack([offs[16 * r : 16 * r + 16].T.reshape(-1) for r in range(8)]).astype(np.int64)
    return lists[np.arange(k) % 512 // 64]


def pack_weight(w):
    k, n = w.shape
    w = f64(np.asarray(w, np.float32).astype(ml_dtypes.bfloat16)).reshape(k // 32, 32, n)
    amax = np.abs(w).max(1)
    byte = np.clip(np.where(amax > 0, np.frexp(amax)[1] - 1 + 127 - 7, 1), 1, 254)
    scaled = (w * np.exp2(127.0 - byte)[:, None, :]).reshape(k, n).astype(np.float32)
    words = np.ascontiguousarray(scaled.reshape(k // 512, 128, 4, n).transpose(0, 1, 3, 2)).astype(ml_dtypes.float8_e4m3fn).view(np.uint8)
    return words, np.ascontiguousarray(byte.astype(np.uint8).reshape(k // 512, 16, n))


def unpack_weight(words, scales):
    g, p, n, _ = words.shape
    vals = np.ascontiguousarray(words).view(ml_dtypes.float8_e4m3fn).astype(np.float64) * np.repeat(np.exp2(scales.astype(np.float64) - 127.0), 8, axis=1)[..., None]
    return vals.transpose(0, 1, 3, 2).reshape(g * 512, n)


def sigmoid(v):
    return 1.0 / (1.0 + np.exp(-np.maximum(v, -700.0)))

def planes(y):
    n, m = y.shape
    v = y.astype(np.float32).astype(ml_dtypes.bfloat16).astype(np.float64).reshape(n // 32, 32, m)
    top = np.abs(v).max(1)
    byte = np.clip(np.where(top > 0, np.frexp(top)[1] - 1 + 127 - 7, 1), 1, 254)
    codes = (v * np.exp2(127.0 - byte)[:, None, :]).reshape(n, m).astype(np.float32).astype(ml_dtypes.float8_e4m3fn).view(np.uint8)
    words = codes.reshape(n // 512, 128, 4, m).transpose(0, 1, 3, 2)
    return np.ascontiguousarray(words), np.ascontiguousarray(byte.astype(np.uint8).reshape(n // 512, 16, m))


K, T, S, G, H, W = 512, 1024, 256, 2048, 512, 128


def setup_inputs():
    n = np.random.standard_normal
    s = mx_kscale(K)[:, None]
    packed_xT = pack_weight(n((K, T)) * s)
    packed_dT = pack_weight(n((K, G)) / s)
    perm = np.random.permutation(S)
    return {
        "x_words": packed_xT[0],
        "x_scales": packed_xT[1],
        "d_words": packed_dT[0],
        "d_scales": packed_dT[1],
        "gs": (np.random.uniform(0.5, 1.5, (K, 1)) * s).astype(np.float32),
        "sl": np.random.uniform(1.0, 2.0, (H, 1)).astype(np.float32),
        "th": (0.5 * n((H, 1))).astype(np.float32),
        "offs": striped8(np.random.randint(0, T, (8, S))),
        "k1": striped8(np.random.randint(0, G, (8, H))),
        "n1": striped(perm[:W]),
        "n2": striped(perm[W:]),
        "n3": striped(np.random.permutation(S)),
        "k2": striped8(np.random.randint(0, G, (8, H))),
        "n4": striped(np.random.permutation(S)),
        "n5": striped(np.random.permutation(S)),
    }


def reference(x_words, x_scales, d_words, d_scales, gs, sl, th, offs, k1, n1, n2, n3, k2, n4, n5):
    d_k2 = unpack_weight(d_words, d_scales)[np.arange(K)[:, None], runs(k2, K)]
    d_k1 = unpack_weight(d_words, d_scales)[np.arange(K)[:, None], runs(k1, K)]
    xq = unpack_weight(x_words, x_scales)[np.arange(K)[:, None], runs(offs, K)]
    h = 0.0625 * (d_k1.T @ xq)
    pa = h[:, unstriped(n1)]
    pb = h[:, unstriped(n2)]
    rb = pa - pb
    ra = pa + pb
    ds = np.zeros((H, S))
    ds[:, unstriped(n1)] = ra
    dt = ds.copy()
    dt[:, unstriped(n2)] = rb
    z = f64(gs) * (np.maximum(dt, dt[:, unstriped(n3)]))
    h2 = 0.0625 * ((d_k2.T @ mxq(z, 0, "e4m3")))
    ds2 = np.zeros((H, S))
    ds2[:, unstriped(n4)] = h2
    sg = sigmoid(f64(sl) * (ds2[:, unstriped(n5)] - f64(th)))
    out_0 = h2 * sg
    return (out_0,) + planes(out_0)

@@ -1,0 +1,198 @@
+from contextlib import ExitStack
+
+import concourse.mybir as mybir
+
+F32 = mybir.dt.float32
+BF16 = mybir.dt.bfloat16
+I32 = mybir.dt.int32
+U32 = mybir.dt.uint32
+U16 = mybir.dt.uint16
+U8 = mybir.dt.uint8
+FP8X4 = mybir.dt.float8_e4m3fn_x4
+ALU = mybir.AluOpType
+ACT = mybir.ActivationFunctionType
+
+P = 128
+K, T, S, G, H, W = 512, 1024, 256, 2048, 512, 128
+PACK = 4
+LANE = 16
+HALF = S // 2
+SIXTEENTH = 0.0625
+
+FLOPS = 2 * (2 * K * H * S)
+
+
+def entries(offsets, start, count):
+    return offsets[:, start // LANE : (start + count) // LANE]
+
+
+def as_words(packed):
+    return packed[0].rearrange("p n t -> p (n t)").bitcast(I32)
+
+
+def tile_picked_hcodehaarherl_none_po_kernel(
+    tc, x_words, x_scales, d_words, d_scales, gs, sl, th, offs, k1, n1, n2, n3, k2, n4, n5, out_0, out_1, out_2
+):
+    nc = tc.nc
+    with ExitStack() as ctx:
+        sb = ctx.enter_context(tc.tile_pool(name="sb", bufs=1))
+        psum = ctx.enter_context(tc.psum_pool(name="psum", bufs=1))
+
+        def tile(shape, dtype, name, tag=None):
+            return sb.tile(shape, dtype, name=name, tag=tag or name, align_bytes=64)
+
+        def load_list(source, name):
+            offsets = tile(list(source.shape), U16, name)
+            nc.sync.dma_start(offsets[:], source)
+            return offsets
+
+        def load_scale_rows(source, width, name):
+            table = tile([P, width], U8, name)
+            rows = source[0].bitcast(I32).unsqueeze(1).to_broadcast([16, 8, width // 4])
+            nc.sync.dma_start(table[:].bitcast(I32), rows)
+            return table
+
+        def load_column(source, name):
+            column = tile([P, PACK], F32, name)
+            nc.gpsimd.dma_start(column[:], source.rearrange("(p t) o -> p (t o)", t=PACK))
+            return column
+
+        def place_scale_rows(picked, width, name, queue):
+            placed = tile([P, width], U8, name)
+            nc.vector.memset(placed[:].bitcast(I32), 0)
+            for q in range(4):
+                queue.dma_start(placed[32 * q : 32 * q + 4, :].bitcast(I32), picked[32 * q : 32 * q + 32 : 8, :].bitcast(I32))
+            return placed
+
+        def deal(dealt, picked):
+            nc.vector.tensor_copy(dealt.rearrange("p (t m) -> p m t", t=PACK), picked.rearrange("p (m t) -> p m t", t=PACK))
+
+        d_table = tile([P, G], U32, "d_table")
+        nc.scalar.dma_start(d_table[:].bitcast(I32), as_words(d_words))
+        x_table = tile([P, T], U32, "x_table")
+        nc.scalar.dma_start(x_table[:].bitcast(I32), as_words(x_words))
+        d_scale_table = load_scale_rows(d_scales, G, "d_scale_table")
+        k1_t = load_list(k1, "k1_t")
+        x_scale_table = load_scale_rows(x_scales, T, "x_scale_table")
+        offs_t = load_list(offs, "offs_t")
+        n1_t = load_list(n1, "n1_t")
+        n2_t = load_list(n2, "n2_t")
+        n3_t = load_list(n3, "n3_t")
+        k2_t = load_list(k2, "k2_t")
+        n4_t = load_list(n4, "n4_t")
+        n5_t = load_list(n5, "n5_t")
+        gs_t = load_column(gs, "gs_t")
+        sl_t = load_column(sl, "sl_t")
+        th_t = load_column(th, "th_t")
+
+        picked_scales = tile([P, H + S], U8, "picked_scales")
+        nc.vector.tensor_copy(picked_scales[:, :H], d_scale_table[:].indirect(k1_t[:]))
+        nc.vector.tensor_copy(picked_scales[:, H:], x_scale_table[:].indirect(offs_t[:]))
+        placed_scales = place_scale_rows(picked_scales, H + S, "placed_scales", nc.scalar)
+        w1_picked = tile([P, H], U32, "w1_picked")
+        nc.vector.tensor_copy(w1_picked[:], d_table[:].indirect(k1_t[:]))
+        w1_words = tile([P, H], U32, "w1_words", tag="held_words")
+        deal(w1_words[:], w1_picked[:])
+        x_picked = tile([P, S], U32, "x_picked")
+        nc.vector.tensor_copy(x_picked[:], x_table[:].indirect(offs_t[:]))
+        w1_scales = tile([P, H], U8, "w1_scales", tag="held_scales")
+
+        h = []
+        for t in range(PACK):
+            cols = slice(P * t, P * (t + 1))
+            nc.vector.tensor_copy(w1_scales[:, cols], placed_scales[:, t:H:PACK])
+            acc = psum.tile([P, S], F32, name=f"acc1_{t}", tag=f"bank{t}")
+            nc.tensor.matmul_mx(
+                acc[:], lhsT=w1_words[:, cols].bitcast(FP8X4), lhsT_scale=w1_scales[:, cols],
+                rhs=x_picked[:].bitcast(FP8X4), rhs_scale=placed_scales[:, H:], start=True, stop=True,
+            )
+            h.append((acc, tile([P, S], F32, f"h{t}")))
+        for acc, h_t in h:
+            nc.vector.tensor_scalar(h_t[:], acc[:], SIXTEENTH, None, ALU.mult)
+
+        dt = []
+        for t in range(PACK):
+            h_t = h[t][1]
+            pa = tile([P, W], F32, f"pa{t}")
+            pb = tile([P, W], F32, f"pb{t}")
+            nc.scalar.activation(pa[:], h_t[:].indirect(n1_t[:]), ACT.Copy)
+            nc.scalar.activation(pb[:], h_t[:].indirect(n2_t[:]), ACT.Copy)
+            ra = tile([P, W], F32, f"ra{t}")
+            rb = tile([P, W], F32, f"rb{t}", tag=f"held_rb{t}")
+            nc.vector.tensor_tensor(ra[:], pa[:], pb[:], ALU.add)
+            nc.vector.tensor_tensor(rb[:], pa[:], pb[:], ALU.subtract)
+            dt.append((ra, rb, tile([P, S], F32, f"dt{t}")))
+        for ra, rb, dt_t in dt:
+            nc.scalar.activation(dt_t[:].indirect(n1_t[:]), ra[:], ACT.Copy)
+        for ra, rb, dt_t in dt:
+            nc.scalar.activation(dt_t[:].indirect(n2_t[:]), rb[:], ACT.Copy)
+
+        w2_picked_scales = tile([P, H], U8, "w2_picked_scales", tag="held_scales")
+        w2_picked = tile([P, H], U32, "w2_picked", tag="held_words")
+        for u in range(2):
+            cols = slice(S * u, S * (u + 1))
+            nc.vector.tensor_copy(w2_picked_scales[:, cols], d_scale_table[:].indirect(entries(k2_t, S * u, S)))
+        w2_placed_scales = place_scale_rows(w2_picked_scales, H, "w2_placed_scales", nc.sync)
+        for u in range(2):
+            cols = slice(S * u, S * (u + 1))
+            nc.vector.tensor_copy(w2_picked[:, cols], d_table[:].indirect(entries(k2_t, S * u, S)))
+        w2_words = tile([P, H], U32, "w2_words")
+        deal(w2_words[:], w2_picked[:])
+        w2_scales = tile([P, H], U8, "w2_scales")
+        deal(w2_scales[:], w2_placed_scales[:])
+        bias = tile([P, PACK], F32, "bias")
+        nc.vector.scalar_tensor_tensor(bias[:], sl_t[:], -1.0, th_t[:], ALU.mult, ALU.mult)
+
+        h2 = [tile([P, S], F32, f"h2_{t}") for t in range(PACK)]
+        ds2 = [tile([P, S], F32, f"ds2_{t}") for t in range(PACK)]
+        for u in range(2):
+            cols = slice(HALF * u, HALF * (u + 1))
+            z_planes = tile([P, PACK, HALF], BF16, f"z_planes{u}")
+            largers = tile([P, PACK, HALF], F32, f"largers{u}", tag="held_z" if u else None)
+            others = tile([P, PACK, HALF], F32, f"others{u}", tag=f"held_rb{PACK - 1}" if u else None)
+            for t in range(PACK):
+                dt_t = dt[t][2]
+                other = others[:, t, :]
+                nc.scalar.activation(other, dt_t[:].indirect(entries(n3_t, HALF * u, HALF)), ACT.Copy)
+                larger = largers[:, t, :]
+                nc.vector.tensor_tensor(larger, dt_t[:, cols], other, ALU.max)
+                nc.vector.tensor_scalar(z_planes[:, t, :], larger, gs_t[:, t : t + 1], None, ALU.mult)
+            z = tile([P, HALF, PACK], BF16, f"z{u}")
+            nc.vector.tensor_copy(z[:], z_planes[:].rearrange("p t c -> p c t"))
+            z_words = tile([P, HALF], U32, f"z_words{u}", tag=None if u else "held_z")
+            z_scales = tile([P, HALF], U8, f"z_scales{u}")
+            nc.vector.quantize_mx(z_words[:].bitcast(FP8X4), z_scales[:], z[:].rearrange("p c t -> p (c t)"))
+            for t in range(PACK):
+                rows = slice(P * t, P * (t + 1))
+                acc = psum.tile([P, HALF], F32, name=f"acc2_{u}_{t}", tag=f"bank{PACK * (1 - u) + t}")
+                nc.tensor.matmul_mx(
+                    acc[:], lhsT=w2_words[:, rows].bitcast(FP8X4), lhsT_scale=w2_scales[:, rows],
+                    rhs=z_words[:].bitcast(FP8X4), rhs_scale=z_scales[:], start=True, stop=True,
+                )
+                nc.vector.tensor_scalar(h2[t][:, cols], acc[:], SIXTEENTH, None, ALU.mult)
+        for u in range(2):
+            cols = slice(HALF * u, HALF * (u + 1))
+            for t in range(PACK):
+                nc.scalar.activation(ds2[t][:].indirect(entries(n4_t, HALF * u, HALF)), h2[t][:, cols], ACT.Copy)
+
+        out_rows = out_0.rearrange("(p t) c -> p t c", t=PACK)
+        out_words = tile([P, S], U32, "out_words")
+        out_scales = tile([P, S], U8, "out_scales")
+        for u in range(2):
+            cols = slice(HALF * u, HALF * (u + 1))
+            result = tile([P, PACK, HALF], F32, f"result{u}")
+            for t in range(PACK):
+                sg = tile([P, HALF], F32, f"sg{u}_{t}")
+                nc.scalar.activation(
+                    sg[:], ds2[t][:].indirect(entries(n5_t, HALF * u, HALF)), ACT.Sigmoid,
+                    bias=bias[:, t : t + 1], scale=sl_t[:, t : t + 1],
+                )
+                nc.vector.tensor_tensor(result[:, t, :], h2[t][:, cols], sg[:], ALU.mult)
+            nc.sync.dma_start(out_rows[:, :, cols], result[:])
+            rounded = tile([P, HALF, PACK], BF16, f"rounded{u}")
+            nc.vector.tensor_copy(rounded[:], result[:].rearrange("p t c -> p c t"))
+            nc.vector.quantize_mx(out_words[:, cols].bitcast(FP8X4), out_scales[:, cols], rounded[:].rearrange("p c t -> p (c t)"))
+            nc.sync.dma_start(as_words(out_1)[:, cols], out_words[:, cols].bitcast(I32))
+        for q in range(4):
+            queue = nc.scalar if q % 2 == 0 else nc.sync
+            queue.dma_start(out_2[0, 4 * q : 4 * q + 4, :].bitcast(I32), out_scales[32 * q : 32 * q + 4, :].bitcast(I32))

@@ -52,51 +52,51 @@ def tile_picked_hcodehaarherl_none_po_kernel(
             nc.sync.dma_start(table[:].bitcast(I32), rows)
             return table
 
-        def load_column(source, name):
-            column = tile([P, PACK], F32, name)
-            nc.gpsimd.dma_start(column[:], source.rearrange("(p t) o -> p (t o)", t=PACK))
+        def load_column(source, column):
+            nc.sync.dma_start(column, source.rearrange("(p t) o -> p (t o)", t=PACK))
             return column
 
-        def place_scale_rows(picked, width, name, queue):
+        def place_scale_rows(picked, width, name, queues):
             placed = tile([P, width], U8, name)
-            nc.vector.memset(placed[:].bitcast(I32), 0)
-            for q in range(4):
-                queue.dma_start(placed[32 * q : 32 * q + 4, :].bitcast(I32), picked[32 * q : 32 * q + 32 : 8, :].bitcast(I32))
+            nc.vector.tensor_copy(placed[:].bitcast(I32), picked[:].bitcast(I32))
+            for r, queue in enumerate(queues, 1):
+                queue.dma_start(placed[r:P:32, :].bitcast(I32), picked[8 * r : P : 32, :].bitcast(I32))
             return placed
 
         def deal(dealt, picked):
             nc.vector.tensor_copy(dealt.rearrange("p (t m) -> p m t", t=PACK), picked.rearrange("p (m t) -> p m t", t=PACK))
 
-        d_table = tile([P, G], U32, "d_table")
-        nc.scalar.dma_start(d_table[:].bitcast(I32), as_words(d_words))
-        x_table = tile([P, T], U32, "x_table")
-        nc.scalar.dma_start(x_table[:].bitcast(I32), as_words(x_words))
-        d_scale_table = load_scale_rows(d_scales, G, "d_scale_table")
-        k1_t = load_list(k1, "k1_t")
         x_scale_table = load_scale_rows(x_scales, T, "x_scale_table")
         offs_t = load_list(offs, "offs_t")
+        d_scale_table = load_scale_rows(d_scales, G, "d_scale_table")
+        k1_t = load_list(k1, "k1_t")
         n1_t = load_list(n1, "n1_t")
         n2_t = load_list(n2, "n2_t")
         n3_t = load_list(n3, "n3_t")
+        d_table = tile([P, G], U32, "d_table")
+        nc.sync.dma_start(d_table[:].bitcast(I32), as_words(d_words))
+        x_table = tile([P, T], U32, "x_table")
+        nc.sync.dma_start(x_table[:].bitcast(I32), as_words(x_words))
         k2_t = load_list(k2, "k2_t")
         n4_t = load_list(n4, "n4_t")
         n5_t = load_list(n5, "n5_t")
-        gs_t = load_column(gs, "gs_t")
-        sl_t = load_column(sl, "sl_t")
-        th_t = load_column(th, "th_t")
 
         picked_scales = tile([P, H + S], U8, "picked_scales")
-        nc.vector.tensor_copy(picked_scales[:, :H], d_scale_table[:].indirect(k1_t[:]))
         nc.vector.tensor_copy(picked_scales[:, H:], x_scale_table[:].indirect(offs_t[:]))
-        placed_scales = place_scale_rows(picked_scales, H + S, "placed_scales", nc.scalar)
+        nc.vector.tensor_copy(picked_scales[:, :H], d_scale_table[:].indirect(k1_t[:]))
+        placed_scales = place_scale_rows(picked_scales, H + S, "placed_scales", (nc.scalar, nc.sync, nc.scalar))
         w1_picked = tile([P, H], U32, "w1_picked")
         nc.vector.tensor_copy(w1_picked[:], d_table[:].indirect(k1_t[:]))
-        w1_words = tile([P, H], U32, "w1_words", tag="held_words")
-        deal(w1_words[:], w1_picked[:])
         x_picked = tile([P, S], U32, "x_picked")
         nc.vector.tensor_copy(x_picked[:], x_table[:].indirect(offs_t[:]))
+        w1_words = tile([P, H], U32, "w1_words", tag="held_words")
+        deal(w1_words[:], w1_picked[:])
         w1_scales = tile([P, H], U8, "w1_scales", tag="held_scales")
 
+        row_values = tile([P, 3, 8], F32, "row_values", tag="picked_scales")
+        gs_t = load_column(gs, row_values[:, 0, :PACK])
+        sl_t = load_column(sl, row_values[:, 1, :PACK])
+        th_t = load_column(th, row_values[:, 2, :PACK])
         h = []
         for t in range(PACK):
             cols = slice(P * t, P * (t + 1))
@@ -132,7 +132,7 @@ def tile_picked_hcodehaarherl_none_po_kernel(
         for u in range(2):
             cols = slice(S * u, S * (u + 1))
             nc.vector.tensor_copy(w2_picked_scales[:, cols], d_scale_table[:].indirect(entries(k2_t, S * u, S)))
-        w2_placed_scales = place_scale_rows(w2_picked_scales, H, "w2_placed_scales", nc.sync)
+        w2_placed_scales = place_scale_rows(w2_picked_scales, H, "w2_placed_scales", (nc.sync, nc.sync, nc.sync))
         for u in range(2):
             cols = slice(S * u, S * (u + 1))
             nc.vector.tensor_copy(w2_picked[:, cols], d_table[:].indirect(entries(k2_t, S * u, S)))
@@ -141,7 +141,7 @@ def tile_picked_hcodehaarherl_none_po_kernel(
         w2_scales = tile([P, H], U8, "w2_scales")
         deal(w2_scales[:], w2_placed_scales[:])
         bias = tile([P, PACK], F32, "bias")
-        nc.vector.scalar_tensor_tensor(bias[:], sl_t[:], -1.0, th_t[:], ALU.mult, ALU.mult)
+        nc.vector.scalar_tensor_tensor(bias[:], sl_t, -1.0, th_t, ALU.mult, ALU.mult)
 
         h2 = [tile([P, S], F32, f"h2_{t}") for t in range(PACK)]
         ds2 = [tile([P, S], F32, f"ds2_{t}") for t in range(PACK)]

@@ -81,6 +81,11 @@ def tile_picked_hcodehaarherl_none_po_kernel(
         n4_t = load_list(n4, "n4_t")
         n5_t = load_list(n5, "n5_t")
 
+        warm_in = tile([P, 1], F32, "warm_in")
+        nc.gpsimd.memset(warm_in[:], 0.0)
+        warm_out = tile([P, 1], F32, "warm_out")
+        nc.scalar.activation(warm_out[:], warm_in[:], ACT.Sigmoid)
+
         picked_scales = tile([P, H + S], U8, "picked_scales")
         nc.vector.tensor_copy(picked_scales[:, H:], x_scale_table[:].indirect(offs_t[:]))
         nc.vector.tensor_copy(picked_scales[:, :H], d_scale_table[:].indirect(k1_t[:]))

@@ -127,10 +127,14 @@ def tile_picked_hcodehaarherl_none_po_kernel(
             nc.vector.tensor_tensor(ra[:], pa[:], pb[:], ALU.add)
             nc.vector.tensor_tensor(rb[:], pa[:], pb[:], ALU.subtract)
             dt.append((ra, rb, tile([P, S], F32, f"dt{t}")))
-        for ra, rb, dt_t in dt:
-            nc.scalar.activation(dt_t[:].indirect(n1_t[:]), ra[:], ACT.Copy)
-        for ra, rb, dt_t in dt:
-            nc.scalar.activation(dt_t[:].indirect(n2_t[:]), rb[:], ACT.Copy)
+        first_others = tile([P, PACK, HALF], F32, "others0")
+        for step in range(PACK + 2):
+            if step < PACK:
+                nc.scalar.activation(dt[step][2][:].indirect(n1_t[:]), dt[step][0][:], ACT.Copy)
+            if 1 <= step <= PACK:
+                nc.scalar.activation(dt[step - 1][2][:].indirect(n2_t[:]), dt[step - 1][1][:], ACT.Copy)
+            if step >= 2:
+                nc.scalar.activation(first_others[:, step - 2, :], dt[step - 2][2][:].indirect(entries(n3_t, 0, HALF)), ACT.Copy)
 
         w2_picked_scales = tile([P, H], U8, "w2_picked_scales", tag="held_scales")
         w2_picked = tile([P, H], U32, "w2_picked", tag="held_words")
@@ -152,18 +156,17 @@ def tile_picked_hcodehaarherl_none_po_kernel(
         ds2 = [tile([P, S], F32, f"ds2_{t}") for t in range(PACK)]
         for u in range(2):
             cols = slice(HALF * u, HALF * (u + 1))
-            z_planes = tile([P, PACK, HALF], BF16, f"z_planes{u}")
+            z = tile([P, HALF, PACK], BF16, f"z{u}")
             largers = tile([P, PACK, HALF], F32, f"largers{u}", tag="held_z" if u else None)
-            others = tile([P, PACK, HALF], F32, f"others{u}", tag=f"held_rb{PACK - 1}" if u else None)
+            others = tile([P, PACK, HALF], F32, "others1", tag=f"held_rb{PACK - 1}") if u else first_others
             for t in range(PACK):
                 dt_t = dt[t][2]
                 other = others[:, t, :]
-                nc.scalar.activation(other, dt_t[:].indirect(entries(n3_t, HALF * u, HALF)), ACT.Copy)
+                if u:
+                    nc.scalar.activation(other, dt_t[:].indirect(entries(n3_t, HALF * u, HALF)), ACT.Copy)
                 larger = largers[:, t, :]
                 nc.vector.tensor_tensor(larger, dt_t[:, cols], other, ALU.max)
-                nc.vector.tensor_scalar(z_planes[:, t, :], larger, gs_t[:, t : t + 1], None, ALU.mult)
-            z = tile([P, HALF, PACK], BF16, f"z{u}")
-            nc.vector.tensor_copy(z[:], z_planes[:].rearrange("p t c -> p c t"))
+                nc.vector.tensor_scalar(z[:, :, t], larger, gs_t[:, t : t + 1], None, ALU.mult)
             z_words = tile([P, HALF], U32, f"z_words{u}", tag=None if u else "held_z")
             z_scales = tile([P, HALF], U8, f"z_scales{u}")
             nc.vector.quantize_mx(z_words[:].bitcast(FP8X4), z_scales[:], z[:].rearrange("p c t -> p (c t)"))

from contextlib import ExitStack

import concourse.mybir as mybir

F32 = mybir.dt.float32
BF16 = mybir.dt.bfloat16
I32 = mybir.dt.int32
U32 = mybir.dt.uint32
U16 = mybir.dt.uint16
U8 = mybir.dt.uint8
FP8X4 = mybir.dt.float8_e4m3fn_x4
ALU = mybir.AluOpType
ACT = mybir.ActivationFunctionType

P = 128
K, T, S, G, H, W = 512, 1024, 256, 2048, 512, 128
PACK = 4
LANE = 16
HALF = S // 2
SIXTEENTH = 0.0625

FLOPS = 2 * (2 * K * H * S)


def entries(offsets, start, count):
    return offsets[:, start // LANE : (start + count) // LANE]


def as_words(packed):
    return packed[0].rearrange("p n t -> p (n t)").bitcast(I32)


def tile_picked_hcodehaarherl_none_po_kernel(
    tc, x_words, x_scales, d_words, d_scales, gs, sl, th, offs, k1, n1, n2, n3, k2, n4, n5, out_0, out_1, out_2
):
    nc = tc.nc
    with ExitStack() as ctx:
        sb = ctx.enter_context(tc.tile_pool(name="sb", bufs=1))
        psum = ctx.enter_context(tc.psum_pool(name="psum", bufs=1))

        def tile(shape, dtype, name, tag=None):
            return sb.tile(shape, dtype, name=name, tag=tag or name, align_bytes=64)

        def load_list(source, name):
            offsets = tile(list(source.shape), U16, name)
            nc.sync.dma_start(offsets[:], source)
            return offsets

        def load_scale_rows(source, width, name):
            table = tile([P, width], U8, name)
            rows = source[0].bitcast(I32).unsqueeze(1).to_broadcast([16, 8, width // 4])
            nc.sync.dma_start(table[:].bitcast(I32), rows)
            return table

        def load_column(source, column):
            nc.sync.dma_start(column, source.rearrange("(p t) o -> p (t o)", t=PACK))
            return column

        def place_scale_rows(picked, width, name, queues):
            placed = tile([P, width], U8, name)
            nc.vector.tensor_copy(placed[:].bitcast(I32), picked[:].bitcast(I32))
            for r, queue in enumerate(queues, 1):
                queue.dma_start(placed[r:P:32, :].bitcast(I32), picked[8 * r : P : 32, :].bitcast(I32))
            return placed

        def deal(dealt, picked):
            nc.vector.tensor_copy(dealt.rearrange("p (t m) -> p m t", t=PACK), picked.rearrange("p (m t) -> p m t", t=PACK))

        x_scale_table = load_scale_rows(x_scales, T, "x_scale_table")
        offs_t = load_list(offs, "offs_t")
        d_scale_table = load_scale_rows(d_scales, G, "d_scale_table")
        k1_t = load_list(k1, "k1_t")
        n1_t = load_list(n1, "n1_t")
        n2_t = load_list(n2, "n2_t")
        n3_t = load_list(n3, "n3_t")
        d_table = tile([P, G], U32, "d_table")
        nc.sync.dma_start(d_table[:].bitcast(I32), as_words(d_words))
        x_table = tile([P, T], U32, "x_table")
        nc.sync.dma_start(x_table[:].bitcast(I32), as_words(x_words))
        k2_t = load_list(k2, "k2_t")
        n4_t = load_list(n4, "n4_t")
        n5_t = load_list(n5, "n5_t")

        warm_in = tile([P, 1], F32, "warm_in")
        nc.gpsimd.memset(warm_in[:], 0.0)
        warm_out = tile([P, 1], F32, "warm_out")
        nc.scalar.activation(warm_out[:], warm_in[:], ACT.Sigmoid)

        picked_scales = tile([P, H + S], U8, "picked_scales")
        nc.vector.tensor_copy(picked_scales[:, H:], x_scale_table[:].indirect(offs_t[:]))
        nc.vector.tensor_copy(picked_scales[:, :H], d_scale_table[:].indirect(k1_t[:]))
        placed_scales = place_scale_rows(picked_scales, H + S, "placed_scales", (nc.scalar, nc.sync, nc.scalar))
        w1_picked = tile([P, H], U32, "w1_picked")
        nc.vector.tensor_copy(w1_picked[:], d_table[:].indirect(k1_t[:]))
        x_picked = tile([P, S], U32, "x_picked")
        nc.vector.tensor_copy(x_picked[:], x_table[:].indirect(offs_t[:]))
        w1_words = tile([P, H], U32, "w1_words", tag="held_words")
        deal(w1_words[:], w1_picked[:])
        w1_scales = tile([P, H], U8, "w1_scales", tag="held_scales")

        row_values = tile([P, 3, 8], F32, "row_values", tag="picked_scales")
        gs_t = load_column(gs, row_values[:, 0, :PACK])
        sl_t = load_column(sl, row_values[:, 1, :PACK])
        th_t = load_column(th, row_values[:, 2, :PACK])
        h = []
        for t in range(PACK):
            cols = slice(P * t, P * (t + 1))
            nc.vector.tensor_copy(w1_scales[:, cols], placed_scales[:, t:H:PACK])
            acc = psum.tile([P, S], F32, name=f"acc1_{t}", tag=f"bank{t}")
            nc.tensor.matmul_mx(
                acc[:], lhsT=w1_words[:, cols].bitcast(FP8X4), lhsT_scale=w1_scales[:, cols],
                rhs=x_picked[:].bitcast(FP8X4), rhs_scale=placed_scales[:, H:], start=True, stop=True,
            )
            h.append((acc, tile([P, S], F32, f"h{t}")))
        for acc, h_t in h:
            nc.vector.tensor_scalar(h_t[:], acc[:], SIXTEENTH, None, ALU.mult)

        dt = []
        for t in range(PACK):
            h_t = h[t][1]
            pa = tile([P, W], F32, f"pa{t}")
            pb = tile([P, W], F32, f"pb{t}")
            nc.scalar.activation(pa[:], h_t[:].indirect(n1_t[:]), ACT.Copy)
            nc.scalar.activation(pb[:], h_t[:].indirect(n2_t[:]), ACT.Copy)
            ra = tile([P, W], F32, f"ra{t}")
            rb = tile([P, W], F32, f"rb{t}", tag=f"held_rb{t}")
            nc.vector.tensor_tensor(ra[:], pa[:], pb[:], ALU.add)
            nc.vector.tensor_tensor(rb[:], pa[:], pb[:], ALU.subtract)
            dt.append((ra, rb, tile([P, S], F32, f"dt{t}")))
        first_others = tile([P, PACK, HALF], F32, "others0")
        for step in range(PACK + 2):
            if step < PACK:
                nc.scalar.activation(dt[step][2][:].indirect(n1_t[:]), dt[step][0][:], ACT.Copy)
            if 1 <= step <= PACK:
                nc.scalar.activation(dt[step - 1][2][:].indirect(n2_t[:]), dt[step - 1][1][:], ACT.Copy)
            if step >= 2:
                nc.scalar.activation(first_others[:, step - 2, :], dt[step - 2][2][:].indirect(entries(n3_t, 0, HALF)), ACT.Copy)

        w2_picked_scales = tile([P, H], U8, "w2_picked_scales", tag="held_scales")
        w2_picked = tile([P, H], U32, "w2_picked", tag="held_words")
        for u in range(2):
            cols = slice(S * u, S * (u + 1))
            nc.vector.tensor_copy(w2_picked_scales[:, cols], d_scale_table[:].indirect(entries(k2_t, S * u, S)))
        w2_placed_scales = place_scale_rows(w2_picked_scales, H, "w2_placed_scales", (nc.sync, nc.sync, nc.sync))
        for u in range(2):
            cols = slice(S * u, S * (u + 1))
            nc.vector.tensor_copy(w2_picked[:, cols], d_table[:].indirect(entries(k2_t, S * u, S)))
        w2_words = tile([P, H], U32, "w2_words")
        deal(w2_words[:], w2_picked[:])
        w2_scales = tile([P, H], U8, "w2_scales")
        deal(w2_scales[:], w2_placed_scales[:])
        bias = tile([P, PACK], F32, "bias")
        nc.vector.scalar_tensor_tensor(bias[:], sl_t, -1.0, th_t, ALU.mult, ALU.mult)

        h2 = [tile([P, S], F32, f"h2_{t}") for t in range(PACK)]
        ds2 = [tile([P, S], F32, f"ds2_{t}") for t in range(PACK)]
        for u in range(2):
            cols = slice(HALF * u, HALF * (u + 1))
            z = tile([P, HALF, PACK], BF16, f"z{u}")
            largers = tile([P, PACK, HALF], F32, f"largers{u}", tag="held_z" if u else None)
            others = tile([P, PACK, HALF], F32, "others1", tag=f"held_rb{PACK - 1}") if u else first_others
            for t in range(PACK):
                dt_t = dt[t][2]
                other = others[:, t, :]
                if u:
                    nc.scalar.activation(other, dt_t[:].indirect(entries(n3_t, HALF * u, HALF)), ACT.Copy)
                larger = largers[:, t, :]
                nc.vector.tensor_tensor(larger, dt_t[:, cols], other, ALU.max)
                nc.vector.tensor_scalar(z[:, :, t], larger, gs_t[:, t : t + 1], None, ALU.mult)
            z_words = tile([P, HALF], U32, f"z_words{u}", tag=None if u else "held_z")
            z_scales = tile([P, HALF], U8, f"z_scales{u}")
            nc.vector.quantize_mx(z_words[:].bitcast(FP8X4), z_scales[:], z[:].rearrange("p c t -> p (c t)"))
            for t in range(PACK):
                rows = slice(P * t, P * (t + 1))
                acc = psum.tile([P, HALF], F32, name=f"acc2_{u}_{t}", tag=f"bank{PACK * (1 - u) + t}")
                nc.tensor.matmul_mx(
                    acc[:], lhsT=w2_words[:, rows].bitcast(FP8X4), lhsT_scale=w2_scales[:, rows],
                    rhs=z_words[:].bitcast(FP8X4), rhs_scale=z_scales[:], start=True, stop=True,
                )
                nc.vector.tensor_scalar(h2[t][:, cols], acc[:], SIXTEENTH, None, ALU.mult)
        for u in range(2):
            cols = slice(HALF * u, HALF * (u + 1))
            for t in range(PACK):
                nc.scalar.activation(ds2[t][:].indirect(entries(n4_t, HALF * u, HALF)), h2[t][:, cols], ACT.Copy)

        out_rows = out_0.rearrange("(p t) c -> p t c", t=PACK)
        out_words = tile([P, S], U32, "out_words")
        out_scales = tile([P, S], U8, "out_scales")
        for u in range(2):
            cols = slice(HALF * u, HALF * (u + 1))
            result = tile([P, PACK, HALF], F32, f"result{u}")
            for t in range(PACK):
                sg = tile([P, HALF], F32, f"sg{u}_{t}")
                nc.scalar.activation(
                    sg[:], ds2[t][:].indirect(entries(n5_t, HALF * u, HALF)), ACT.Sigmoid,
                    bias=bias[:, t : t + 1], scale=sl_t[:, t : t + 1],
                )
                nc.vector.tensor_tensor(result[:, t, :], h2[t][:, cols], sg[:], ALU.mult)
            nc.sync.dma_start(out_rows[:, :, cols], result[:])
            rounded = tile([P, HALF, PACK], BF16, f"rounded{u}")
            nc.vector.tensor_copy(rounded[:], result[:].rearrange("p t c -> p c t"))
            nc.vector.quantize_mx(out_words[:, cols].bitcast(FP8X4), out_scales[:, cols], rounded[:].rearrange("p c t -> p (c t)"))
            nc.sync.dma_start(as_words(out_1)[:, cols], out_words[:, cols].bitcast(I32))
        for q in range(4):
            queue = nc.scalar if q % 2 == 0 else nc.sync
            queue.dma_start(out_2[0, 4 * q : 4 * q + 4, :].bitcast(I32), out_scales[32 * q : 32 * q + 4, :].bitcast(I32))
